import numpy as np
import ml_dtypes


def mxq(x, axis, fmt="e4m3"):
    dtype, down = {"e4m3": (ml_dtypes.float8_e4m3fn, 7), "e5m2": (ml_dtypes.float8_e5m2, 14)}[fmt]
    v = np.moveaxis(np.asarray(x, np.float32).astype(ml_dtypes.bfloat16).astype(np.float64), axis, -1)
    blocks = v.reshape(v.shape[:-1] + (-1, 32))
    amax = np.abs(blocks).max(-1, keepdims=True)
    byte = np.maximum(np.where(amax > 0, np.frexp(amax)[1] - 1 + 127, 0) - down, 1)
    scale = np.exp2(byte - 127.0)
    codes = (blocks / scale).astype(np.float32).astype(dtype).astype(np.float64)
    return np.moveaxis((codes * scale).reshape(v.shape), -1, axis)


WIDE = False


def mx_kscale(k):
    if not WIDE:
        return np.ones(k)
    levels = np.array([10, -10, 5, -5, 0])
    if k % 512:
        return np.exp2(np.random.permutation(np.resize(levels, k // 32))).repeat(32)
    a = np.empty((k // 512, 16))
    for p in range(k // 512):
        a[p, :8] = np.random.permutation(np.resize(levels, 8))
        for g in range(8):
            far = levels[np.abs(levels - a[p, g]) >= 10]
            a[p, g + 8] = far[np.random.randint(len(far))]
    return np.exp2(a.ravel()).repeat(32)


def f64(x):
    return np.asarray(x).astype(np.float64)


def striped(idx):
    return np.tile(idx.reshape(-1, 16).T, (8, 1)).astype(np.uint16)


def unstriped(offs):
    return offs[:16].T.reshape(-1).astype(np.int64)


K, T, E, C, N = 1024, 1280, 8, 128, 512
M = 384


def by_expert(wq, xq):
    return np.concatenate([wq[e].T @ xq[:, e * C:(e + 1) * C] for e in range(E)], axis=1)


def setup_inputs():
    n = np.random.standard_normal
    s = mx_kscale(K)[:, None]
    v = mx_kscale(N)
    return {
        "xT": (n((K, T)) * s).astype(np.float32),
        "w": (n((E, K, N)) / np.sqrt(K) / s[None] * v[None, None, :]).astype(np.float32),
        "wp": (n((N, M)) / np.sqrt(N) / v[:, None]).astype(np.float32),
        "gate": np.tile(np.random.uniform(0.2, 1.0, E * C), (N, 1)).astype(np.float32),
        "offs": striped(np.random.permutation(T)[:E * C]),
    }


def reference(xT, w, wp, gate, offs):
    idx = unstriped(offs)
    xq = mxq(f64(xT)[:, idx], 0, "e4m3")
    y = by_expert(mxq(f64(w), 1, "e4m3"), xq)
    c = np.zeros((N, T))
    c[:, idx] = f64(gate) * y
    return mxq(f64(wp), 0, "e4m3").T @ mxq(c, 0, "e4m3")

@@ -1,0 +1,278 @@
+from contextlib import ExitStack
+
+import concourse.mybir as mybir
+
+K, T, E, C, N, M = 1024, 1280, 8, 128, 512, 384
+SLOTS = E * C
+FLOPS = 2 * SLOTS * K * N + 2 * T * N * M
+BYTES = 4 * (K * T + E * K * N + N * M + SLOTS + M * T) + 2 * SLOTS
+
+F32 = mybir.dt.float32
+BF16 = mybir.dt.bfloat16
+U32 = mybir.dt.uint32
+U16 = mybir.dt.uint16
+U8 = mybir.dt.uint8
+FP8X4 = mybir.dt.float8_e4m3fn_x4
+ADD = mybir.AluOpType.add
+MULT = mybir.AluOpType.mult
+COPY = mybir.ActivationFunctionType.Copy
+
+P = 128
+PACK = 4
+KP = P * PACK
+PASSES = K // KP
+GATHER = 512
+XRAW = 4
+XBF = 3
+WRAW = 6
+WBF = 4
+WQ = 6
+W_ENGINE = 'vssssvssssvsssss'
+GROUP_OF = {0: (0, 0, 2), 1: (0, 0, 2), 2: (1, 2, 2), 3: (1, 2, 2), 4: (2, 4, 2), 5: (2, 4, 2), 6: (3, 6, 1), 7: (4, 7, 1)}
+
+
+def tile_moe_nxt_lin_none_kernel(tc, xT, w, wp, gate, offs, out):
+    nc = tc.nc
+    with ExitStack() as ctx:
+        keep = ctx.enter_context(tc.tile_pool(name="keep", bufs=1))
+        xraw = ctx.enter_context(tc.tile_pool(name="xraw", bufs=XRAW))
+        xbf = ctx.enter_context(tc.tile_pool(name="xbf", bufs=XBF))
+        wraw = ctx.enter_context(tc.tile_pool(name="wraw", bufs=WRAW))
+        wbf = ctx.enter_context(tc.tile_pool(name="wbf", bufs=WBF))
+        wq = ctx.enter_context(tc.tile_pool(name="wq", bufs=WQ))
+        cpool = ctx.enter_context(tc.tile_pool(name="c", bufs=2))
+        ypsum = ctx.enter_context(tc.psum_pool(name="ypsum", bufs=3))
+        opsum = ctx.enter_context(tc.psum_pool(name="opsum", bufs=2))
+
+        offsets = keep.tile([P, SLOTS // 16], U16, name="offsets")
+        nc.sync.dma_start(offsets[:], offs)
+
+        xcodes = [keep.tile([P, T], U32, align_bytes=64, name="xcodes%d" % a) for a in range(PASSES)]
+        xscales = keep.tile([P, T], U8, align_bytes=64, name="xscales")
+        gcodes = [keep.tile([P, SLOTS], U32, align_bytes=64, name="gcodes%d" % a) for a in range(PASSES)]
+        gscales = keep.tile([P, SLOTS], U8, align_bytes=64, name="gscales")
+        gates = keep.tile([P, SLOTS], F32, name="gates")
+        wpraw = keep.tile([P, PACK, M], F32, name="wpraw")
+        wpbf = keep.tile([P, M, PACK], BF16, align_bytes=64, name="wpbf")
+        wpcodes = keep.tile([P, M], U32, align_bytes=64, name="wpcodes")
+        wpscales = keep.tile([P, M], U8, align_bytes=64, name="wpscales")
+        oslots = keep.tile([P, M // P, SLOTS], F32, name="oslots")
+        windows = [keep.tile([P, T], F32, name="window%d" % f) for f in range(M // P)]
+
+        nc.gpsimd.memset(xscales[:], 0)
+        for f in range(M // P):
+            nc.gpsimd.memset(windows[f][:], 0.0)
+
+        raw_tiles = {}
+        grouped_tiles = {}
+        quantized = {}
+
+        def load_w(e, a):
+            raw = wraw.tile([P, PACK, N], F32, name="raw")
+            nc.sync.dma_start(raw[:], w[e, a * KP:(a + 1) * KP, :].rearrange("(p j) n -> p j n", j=PACK))
+            raw_tiles[e, a] = raw
+
+        def copy(engine, dst, src):
+            if engine == "v":
+                nc.vector.tensor_copy(out=dst, in_=src)
+            elif engine == "g":
+                nc.gpsimd.tensor_scalar(out=dst, in0=src, scalar1=1.0, scalar2=0.0, op0=MULT, op1=ADD)
+            else:
+                nc.scalar.activation(out=dst, in_=src, func=COPY)
+
+        def group_w(e, a):
+            grouped = wbf.tile([P, N * PACK], BF16, align_bytes=64, name="grouped")
+            dst = grouped[:].rearrange("p (t m j) -> p m j t", t=PACK, j=PACK)
+            src = raw_tiles.pop((e, a))[:].rearrange("p j (m t) -> p m j t", t=PACK)
+            copy(W_ENGINE[e * PASSES + a], dst, src)
+            grouped_tiles[e, a] = grouped
+
+        def quantize_w(e, a):
+            codes = wq.tile([P, N], U32, align_bytes=64, name="codes")
+            scales = wq.tile([P, N], U8, align_bytes=64, name="scales")
+            nc.vector.quantize_mx(out=codes[:].bitcast(FP8X4), scales=scales[:], in_=grouped_tiles.pop((e, a))[:])
+            quantized[e, a] = codes, scales
+
+        def tokens(a, t0, t1, engine):
+            xr = xraw.tile([P, PACK, t1 - t0], F32, name="xr")
+            nc.sync.dma_start(xr[:], xT[a * KP:(a + 1) * KP, t0:t1].rearrange("(p j) t -> p j t", j=PACK))
+            xb = xbf.tile([P, (t1 - t0) * PACK], BF16, align_bytes=64, name="xb")
+            copy(
+                engine,
+                xb[:].rearrange("p (c i j) -> p c j i", i=4, j=PACK),
+                xr[:].rearrange("p j (c i) -> p c j i", i=4),
+            )
+            nc.vector.quantize_mx(
+                out=xcodes[a][:, t0:t1].bitcast(FP8X4), scales=xscales[PACK * a:P, t0:t1], in_=xb[:]
+            )
+
+        gather_parts = [slice(g * GATHER // 16, (g + 1) * GATHER // 16) for g in range(SLOTS // GATHER)]
+
+        def gather_codes(a):
+            for g, cols in enumerate(gather_parts):
+                nc.vector.tensor_copy(
+                    out=gcodes[a][:, g * GATHER:(g + 1) * GATHER], in_=xcodes[a][:].indirect(offsets[:, cols])
+                )
+
+        def gather_scales():
+            for g, cols in enumerate(gather_parts):
+                nc.vector.tensor_copy(
+                    out=gscales[:, g * GATHER:(g + 1) * GATHER], in_=xscales[:].indirect(offsets[:, cols])
+                )
+
+        def load_gate():
+            nc.sync.dma_start(gates[:], gate[0:P, :])
+
+        def load_wp():
+            nc.sync.dma_start(wpraw[:], wp.rearrange("(q r) f -> q r f", r=PACK))
+
+        def group_wp(engine):
+            copy(
+                engine,
+                wpbf[:].rearrange("q (c i) r -> q c r i", i=4),
+                wpraw[:].rearrange("q r (c i) -> q c r i", i=4),
+            )
+            for f0, f1 in ((0, 256), (256, 384)):
+                nc.vector.quantize_mx(
+                    out=wpcodes[:, f0:f1].bitcast(FP8X4),
+                    scales=wpscales[:, f0:f1],
+                    in_=wpbf[:, f0:f1, :].rearrange("p f r -> p (f r)"),
+                )
+
+        group_cb = {}
+
+        def experts(e):
+            y = ypsum.tile([P, PACK, C], F32, name="y")
+            for t in range(PACK):
+                for a in range(PASSES):
+                    codes, scales = quantized[e, a]
+                    nc.tensor.matmul_mx(
+                        out=y[:, t, :],
+                        lhsT=codes[:, t * P:(t + 1) * P].bitcast(FP8X4),
+                        lhsT_scale=scales[:, t * P:(t + 1) * P],
+                        rhs=gcodes[a][:, e * C:(e + 1) * C].bitcast(FP8X4),
+                        rhs_scale=gscales[PACK * a:P, e * C:(e + 1) * C],
+                        start=(a == 0),
+                        stop=(a == PASSES - 1),
+                    )
+            gi, first, size = GROUP_OF[e]
+            if e == first:
+                cb = cpool.tile([P, size * C, PACK], BF16, align_bytes=64, name="cb")
+                group_cb[gi] = cb
+            i = e - first
+            nc.vector.tensor_tensor(
+                out=group_cb[gi][:, i * C:(i + 1) * C, :],
+                in0=y[:].rearrange("p t s -> p s t"),
+                in1=gates[:, e * C:(e + 1) * C].unsqueeze(2).to_broadcast([P, C, PACK]),
+                op=MULT,
+            )
+
+        def project(first, size):
+            width = size * C
+            s0 = first * C
+            cb = group_cb[GROUP_OF[first][0]]
+            ccodes = cpool.tile([P, width], U32, align_bytes=64, name="ccodes")
+            cscales = cpool.tile([P, width], U8, align_bytes=64, name="cscales")
+            nc.vector.quantize_mx(
+                out=ccodes[:].bitcast(FP8X4), scales=cscales[:], in_=cb[:].rearrange("p s r -> p (s r)")
+            )
+            o = opsum.tile([P, 4, 2 * C], F32, name="o")
+            for f in range(M // P):
+                nc.tensor.matmul_mx(
+                    out=o[:, f, 0:width],
+                    lhsT=wpcodes[:, f * P:(f + 1) * P].bitcast(FP8X4),
+                    lhsT_scale=wpscales[:, f * P:(f + 1) * P],
+                    rhs=ccodes[:].bitcast(FP8X4),
+                    rhs_scale=cscales[:],
+                    start=True,
+                    stop=True,
+                )
+            nc.scalar.activation(out=oslots[:, 0:2, s0:s0 + width], in_=o[:, 0:2, 0:width], func=COPY)
+            nc.scalar.activation(out=oslots[:, 2, s0:s0 + width], in_=o[:, 2, 0:width], func=COPY)
+
+        def scatter(a0, a1):
+            for f in range(M // P):
+                nc.vector.tensor_copy(
+                    out=windows[f][:].indirect(offsets[:, a0 // 16:a1 // 16]), in_=oslots[:, f, a0:a1]
+                )
+
+        tokens(0, 0, 256, 's')
+        tokens(0, 256, 768, 'v')
+        tokens(0, 768, 1280, 'v')
+        gather_codes(0)
+        tokens(1, 0, 512, 's')
+        load_w(0, 0)
+        group_w(0, 0)
+        load_w(0, 1)
+        group_w(0, 1)
+        tokens(1, 512, 1024, 's')
+        tokens(1, 1024, 1280, 'v')
+        load_w(1, 0)
+        load_w(1, 1)
+        load_gate()
+        load_wp()
+        load_w(2, 0)
+        gather_codes(1)
+        gather_scales()
+        quantize_w(0, 0)
+        quantize_w(0, 1)
+        group_w(1, 0)
+        load_w(2, 1)
+        load_w(3, 0)
+        group_w(1, 1)
+        load_w(3, 1)
+        group_wp('s')
+        experts(0)
+        quantize_w(1, 0)
+        quantize_w(1, 1)
+        group_w(2, 0)
+        load_w(4, 0)
+        group_w(2, 1)
+        load_w(4, 1)
+        experts(1)
+        project(0, 2)
+        quantize_w(2, 0)
+        quantize_w(2, 1)
+        group_w(3, 0)
+        load_w(5, 0)
+        group_w(3, 1)
+        load_w(5, 1)
+        experts(2)
+        quantize_w(3, 0)
+        quantize_w(3, 1)
+        scatter(0, 256)
+        group_w(4, 0)
+        load_w(6, 0)
+        group_w(4, 1)
+        load_w(6, 1)
+        experts(3)
+        project(2, 2)
+        quantize_w(4, 0)
+        quantize_w(4, 1)
+        group_w(5, 0)
+        load_w(7, 0)
+        group_w(5, 1)
+        load_w(7, 1)
+        experts(4)
+        quantize_w(5, 0)
+        quantize_w(5, 1)
+        scatter(256, 512)
+        group_w(6, 0)
+        group_w(6, 1)
+        experts(5)
+        project(4, 2)
+        quantize_w(6, 0)
+        quantize_w(6, 1)
+        group_w(7, 0)
+        group_w(7, 1)
+        experts(6)
+        project(6, 1)
+        quantize_w(7, 0)
+        quantize_w(7, 1)
+        experts(7)
+        project(7, 1)
+        scatter(512, 704)
+        scatter(704, 864)
+        scatter(864, 1024)
+        for f in range(M // P):
+            nc.sync.dma_start(out[f * P:(f + 1) * P, :], windows[f][:])

@@ -22,12 +22,16 @@ PACK = 4
 KP = P * PACK
 PASSES = K // KP
 GATHER = 512
-XRAW = 4
-XBF = 3
-WRAW = 6
-WBF = 4
-WQ = 6
-W_ENGINE = 'vssssvssssvsssss'
+XRAW, XBF, WRAW, WBF, WQ = 4, 3, 5, 4, 4
+X_CHUNKS = ((0, 0, 256), (0, 256, 768), (0, 768, 1280), (1, 0, 512), (1, 512, 1024), (1, 1024, 1280))
+X_ENGINE = 'vvsvsv'
+W_ENGINE = 'ssssssssssssssss'
+WP_ENGINE = 's'
+LAST_ENGINE = 'sssssssssssssss'
+GROUPS = ((0, 2), (2, 2), (4, 2), (6, 1), (7, 1))
+CUTS = ((0, 256), (256, 512), (512, 704), (704, 864), (864, 1024))
+TURN_ENGINE = 'ssssssss'
+SPLIT = {"p": 192, "q": 128, "r": 256}
 GROUP_OF = {0: (0, 0, 2), 1: (0, 0, 2), 2: (1, 2, 2), 3: (1, 2, 2), 4: (2, 4, 2), 5: (2, 4, 2), 6: (3, 6, 1), 7: (4, 7, 1)}
 
 
@@ -56,21 +60,22 @@ def tile_moe_nxt_lin_none_kernel(tc, xT, w, wp, gate, offs, out):
         wpbf = keep.tile([P, M, PACK], BF16, align_bytes=64, name="wpbf")
         wpcodes = keep.tile([P, M], U32, align_bytes=64, name="wpcodes")
         wpscales = keep.tile([P, M], U8, align_bytes=64, name="wpscales")
-        oslots = keep.tile([P, M // P, SLOTS], F32, name="oslots")
+        oslots = [keep.tile([P, SLOTS], F32, name="oslots%d" % f) for f in range(M // P)]
         windows = [keep.tile([P, T], F32, name="window%d" % f) for f in range(M // P)]
 
         nc.gpsimd.memset(xscales[:], 0)
         for f in range(M // P):
             nc.gpsimd.memset(windows[f][:], 0.0)
 
+        x_tiles = {}
+        x_parts = {}
         raw_tiles = {}
         grouped_tiles = {}
         quantized = {}
-
-        def load_w(e, a):
-            raw = wraw.tile([P, PACK, N], F32, name="raw")
-            nc.sync.dma_start(raw[:], w[e, a * KP:(a + 1) * KP, :].rearrange("(p j) n -> p j n", j=PACK))
-            raw_tiles[e, a] = raw
+        products = {}
+        gated = {}
+        ccodes_of = {}
+        projected = {}
 
         def copy(engine, dst, src):
             if engine == "v":
@@ -80,72 +85,85 @@ def tile_moe_nxt_lin_none_kernel(tc, xT, w, wp, gate, offs, out):
             else:
                 nc.scalar.activation(out=dst, in_=src, func=COPY)
 
-        def group_w(e, a):
-            grouped = wbf.tile([P, N * PACK], BF16, align_bytes=64, name="grouped")
-            dst = grouped[:].rearrange("p (t m j) -> p m j t", t=PACK, j=PACK)
-            src = raw_tiles.pop((e, a))[:].rearrange("p j (m t) -> p m j t", t=PACK)
-            copy(W_ENGINE[e * PASSES + a], dst, src)
-            grouped_tiles[e, a] = grouped
-
-        def quantize_w(e, a):
-            codes = wq.tile([P, N], U32, align_bytes=64, name="codes")
-            scales = wq.tile([P, N], U8, align_bytes=64, name="scales")
-            nc.vector.quantize_mx(out=codes[:].bitcast(FP8X4), scales=scales[:], in_=grouped_tiles.pop((e, a))[:])
-            quantized[e, a] = codes, scales
-
-        def tokens(a, t0, t1, engine):
+        def LX(i):
+            a, t0, t1 = X_CHUNKS[i]
             xr = xraw.tile([P, PACK, t1 - t0], F32, name="xr")
             nc.sync.dma_start(xr[:], xT[a * KP:(a + 1) * KP, t0:t1].rearrange("(p j) t -> p j t", j=PACK))
+            x_parts[i] = xr
+
+        def GX(i):
+            a, t0, t1 = X_CHUNKS[i]
             xb = xbf.tile([P, (t1 - t0) * PACK], BF16, align_bytes=64, name="xb")
             copy(
-                engine,
+                X_ENGINE[i],
                 xb[:].rearrange("p (c i j) -> p c j i", i=4, j=PACK),
-                xr[:].rearrange("p j (c i) -> p c j i", i=4),
+                x_parts.pop(i)[:].rearrange("p j (c i) -> p c j i", i=4),
             )
+            x_tiles[i] = xb
+
+        def QX(i):
+            a, t0, t1 = X_CHUNKS[i]
             nc.vector.quantize_mx(
-                out=xcodes[a][:, t0:t1].bitcast(FP8X4), scales=xscales[PACK * a:P, t0:t1], in_=xb[:]
+                out=xcodes[a][:, t0:t1].bitcast(FP8X4), scales=xscales[PACK * a:P, t0:t1], in_=x_tiles.pop(i)[:]
             )
 
-        gather_parts = [slice(g * GATHER // 16, (g + 1) * GATHER // 16) for g in range(SLOTS // GATHER)]
+        def GA(a, g):
+            nc.vector.tensor_copy(
+                out=gcodes[a][:, g * GATHER:(g + 1) * GATHER],
+                in_=xcodes[a][:].indirect(offsets[:, g * GATHER // 16:(g + 1) * GATHER // 16]),
+            )
 
-        def gather_codes(a):
-            for g, cols in enumerate(gather_parts):
-                nc.vector.tensor_copy(
-                    out=gcodes[a][:, g * GATHER:(g + 1) * GATHER], in_=xcodes[a][:].indirect(offsets[:, cols])
-                )
+        def GS(g):
+            nc.vector.tensor_copy(
+                out=gscales[:, g * GATHER:(g + 1) * GATHER],
+                in_=xscales[:].indirect(offsets[:, g * GATHER // 16:(g + 1) * GATHER // 16]),
+            )
 
-        def gather_scales():
-            for g, cols in enumerate(gather_parts):
-                nc.vector.tensor_copy(
-                    out=gscales[:, g * GATHER:(g + 1) * GATHER], in_=xscales[:].indirect(offsets[:, cols])
-                )
-
-        def load_gate():
+        def LG():
             nc.sync.dma_start(gates[:], gate[0:P, :])
 
-        def load_wp():
+        def LP():
             nc.sync.dma_start(wpraw[:], wp.rearrange("(q r) f -> q r f", r=PACK))
 
-        def group_wp(engine):
+        def GP():
             copy(
-                engine,
+                WP_ENGINE,
                 wpbf[:].rearrange("q (c i) r -> q c r i", i=4),
                 wpraw[:].rearrange("q r (c i) -> q c r i", i=4),
             )
-            for f0, f1 in ((0, 256), (256, 384)):
-                nc.vector.quantize_mx(
-                    out=wpcodes[:, f0:f1].bitcast(FP8X4),
-                    scales=wpscales[:, f0:f1],
-                    in_=wpbf[:, f0:f1, :].rearrange("p f r -> p (f r)"),
-                )
 
-        group_cb = {}
+        def QP(i):
+            f0, f1 = ((0, 256), (256, 384))[i]
+            nc.vector.quantize_mx(
+                out=wpcodes[:, f0:f1].bitcast(FP8X4),
+                scales=wpscales[:, f0:f1],
+                in_=wpbf[:, f0:f1, :].rearrange("p f r -> p (f r)"),
+            )
 
-        def experts(e):
+        def LW(k):
+            e, a = divmod(k, PASSES)
+            raw = wraw.tile([P, PACK, N], F32, name="raw")
+            nc.sync.dma_start(raw[:], w[e, a * KP:(a + 1) * KP, :].rearrange("(p j) n -> p j n", j=PACK))
+            raw_tiles[k] = raw
+
+        def GW(k):
+            grouped = wbf.tile([P, N * PACK], BF16, align_bytes=64, name="grouped")
+            dst = grouped[:].rearrange("p (t m j) -> p m j t", t=PACK, j=PACK)
+            src = raw_tiles.pop(k)[:].rearrange("p j (m t) -> p m j t", t=PACK)
+            copy(W_ENGINE[k], dst, src)
+            grouped_tiles[k] = grouped
+
+        def QW(k):
+            codes = wq.tile([P, N], U32, align_bytes=64, name="codes")
+            scales = wq.tile([P, N], U8, align_bytes=64, name="scales")
+            nc.vector.quantize_mx(out=codes[:].bitcast(FP8X4), scales=scales[:], in_=grouped_tiles.pop(k)[:])
+            quantized[k] = codes, scales
+
+        def MM(e):
             y = ypsum.tile([P, PACK, C], F32, name="y")
             for t in range(PACK):
                 for a in range(PASSES):
-                    codes, scales = quantized[e, a]
+                    codes, scales = quantized[e * PASSES + a]
                     nc.tensor.matmul_mx(
                         out=y[:, t, :],
                         lhsT=codes[:, t * P:(t + 1) * P].bitcast(FP8X4),
@@ -155,27 +173,33 @@ def tile_moe_nxt_lin_none_kernel(tc, xT, w, wp, gate, offs, out):
                         start=(a == 0),
                         stop=(a == PASSES - 1),
                     )
+            products[e] = y
+
+        def GT(e):
             gi, first, size = GROUP_OF[e]
-            if e == first:
+            if gi not in gated:
                 cb = cpool.tile([P, size * C, PACK], BF16, align_bytes=64, name="cb")
-                group_cb[gi] = cb
+                gated[gi] = cb
             i = e - first
             nc.vector.tensor_tensor(
-                out=group_cb[gi][:, i * C:(i + 1) * C, :],
-                in0=y[:].rearrange("p t s -> p s t"),
+                out=gated[gi][:, i * C:(i + 1) * C, :],
+                in0=products.pop(e)[:].rearrange("p t s -> p s t"),
                 in1=gates[:, e * C:(e + 1) * C].unsqueeze(2).to_broadcast([P, C, PACK]),
                 op=MULT,
             )
 
-        def project(first, size):
-            width = size * C
-            s0 = first * C
-            cb = group_cb[GROUP_OF[first][0]]
+        def QC(gi):
+            width = GROUPS[gi][1] * C
             ccodes = cpool.tile([P, width], U32, align_bytes=64, name="ccodes")
             cscales = cpool.tile([P, width], U8, align_bytes=64, name="cscales")
             nc.vector.quantize_mx(
-                out=ccodes[:].bitcast(FP8X4), scales=cscales[:], in_=cb[:].rearrange("p s r -> p (s r)")
+                out=ccodes[:].bitcast(FP8X4), scales=cscales[:], in_=gated[gi][:].rearrange("p s r -> p (s r)")
             )
+            ccodes_of[gi] = ccodes, cscales
+
+        def PM(gi):
+            width = GROUPS[gi][1] * C
+            ccodes, cscales = ccodes_of.pop(gi)
             o = opsum.tile([P, 4, 2 * C], F32, name="o")
             for f in range(M // P):
                 nc.tensor.matmul_mx(
@@ -187,92 +211,155 @@ def tile_moe_nxt_lin_none_kernel(tc, xT, w, wp, gate, offs, out):
                     start=True,
                     stop=True,
                 )
-            nc.scalar.activation(out=oslots[:, 0:2, s0:s0 + width], in_=o[:, 0:2, 0:width], func=COPY)
-            nc.scalar.activation(out=oslots[:, 2, s0:s0 + width], in_=o[:, 2, 0:width], func=COPY)
+            projected[gi] = o
 
-        def scatter(a0, a1):
-            for f in range(M // P):
-                nc.vector.tensor_copy(
-                    out=windows[f][:].indirect(offsets[:, a0 // 16:a1 // 16]), in_=oslots[:, f, a0:a1]
-                )
+        def EV(gi, f):
+            first, size = GROUPS[gi]
+            s0, s1 = first * C, (first + size) * C
+            copy(LAST_ENGINE[gi * 3 + f], oslots[f][:, s0:s1], projected[gi][:, f, 0:s1 - s0])
 
-        tokens(0, 0, 256, 's')
-        tokens(0, 256, 768, 'v')
-        tokens(0, 768, 1280, 'v')
-        gather_codes(0)
-        tokens(1, 0, 512, 's')
-        load_w(0, 0)
-        group_w(0, 0)
-        load_w(0, 1)
-        group_w(0, 1)
-        tokens(1, 512, 1024, 's')
-        tokens(1, 1024, 1280, 'v')
-        load_w(1, 0)
-        load_w(1, 1)
-        load_gate()
-        load_wp()
-        load_w(2, 0)
-        gather_codes(1)
-        gather_scales()
-        quantize_w(0, 0)
-        quantize_w(0, 1)
-        group_w(1, 0)
-        load_w(2, 1)
-        load_w(3, 0)
-        group_w(1, 1)
-        load_w(3, 1)
-        group_wp('s')
-        experts(0)
-        quantize_w(1, 0)
-        quantize_w(1, 1)
-        group_w(2, 0)
-        load_w(4, 0)
-        group_w(2, 1)
-        load_w(4, 1)
-        experts(1)
-        project(0, 2)
-        quantize_w(2, 0)
-        quantize_w(2, 1)
-        group_w(3, 0)
-        load_w(5, 0)
-        group_w(3, 1)
-        load_w(5, 1)
-        experts(2)
-        quantize_w(3, 0)
-        quantize_w(3, 1)
-        scatter(0, 256)
-        group_w(4, 0)
-        load_w(6, 0)
-        group_w(4, 1)
-        load_w(6, 1)
-        experts(3)
-        project(2, 2)
-        quantize_w(4, 0)
-        quantize_w(4, 1)
-        group_w(5, 0)
-        load_w(7, 0)
-        group_w(5, 1)
-        load_w(7, 1)
-        experts(4)
-        quantize_w(5, 0)
-        quantize_w(5, 1)
-        scatter(256, 512)
-        group_w(6, 0)
-        group_w(6, 1)
-        experts(5)
-        project(4, 2)
-        quantize_w(6, 0)
-        quantize_w(6, 1)
-        group_w(7, 0)
-        group_w(7, 1)
-        experts(6)
-        project(6, 1)
-        quantize_w(7, 0)
-        quantize_w(7, 1)
-        experts(7)
-        project(7, 1)
-        scatter(512, 704)
-        scatter(704, 864)
-        scatter(864, 1024)
-        for f in range(M // P):
+        def SC(i, f):
+            a0, a1 = CUTS[i]
+            nc.vector.tensor_copy(
+                out=windows[f][:].indirect(offsets[:, a0 // 16:a1 // 16]), in_=oslots[f][:, a0:a1]
+            )
+
+        def ST(f):
             nc.sync.dma_start(out[f * P:(f + 1) * P, :], windows[f][:])
+
+        LX(0)
+        GX(0)
+        QX(0)
+        LX(2)
+        GX(2)
+        QX(2)
+        LX(1)
+        GX(1)
+        QX(1)
+        GA(0, 0)
+        GA(0, 1)
+        LX(4)
+        GX(4)
+        QX(4)
+        LX(3)
+        GX(3)
+        QX(3)
+        LW(0)
+        GW(0)
+        LX(5)
+        GX(5)
+        QX(5)
+        GA(1, 0)
+        GA(1, 1)
+        LW(1)
+        LG()
+        LP()
+        LW(2)
+        LW(3)
+        LW(4)
+        GS(0)
+        GS(1)
+        GW(1)
+        QW(0)
+        QW(1)
+        GW(2)
+        GW(3)
+        LW(5)
+        GP()
+        QP(0)
+        QP(1)
+        MM(0)
+        GT(0)
+        QW(2)
+        QW(3)
+        GW(4)
+        LW(6)
+        GW(5)
+        LW(7)
+        MM(1)
+        GT(1)
+        QW(4)
+        QW(5)
+        QC(0)
+        PM(0)
+        EV(0, 0)
+        EV(0, 1)
+        EV(0, 2)
+        GW(6)
+        LW(8)
+        GW(7)
+        LW(9)
+        MM(2)
+        GT(2)
+        QW(6)
+        QW(7)
+        GW(8)
+        LW(10)
+        GW(9)
+        LW(11)
+        MM(3)
+        GT(3)
+        QW(8)
+        QW(9)
+        QC(1)
+        PM(1)
+        EV(1, 0)
+        EV(1, 1)
+        EV(1, 2)
+        GW(10)
+        LW(12)
+        GW(11)
+        LW(13)
+        MM(4)
+        GT(4)
+        QW(10)
+        QW(11)
+        SC(0, 0)
+        SC(0, 1)
+        SC(0, 2)
+        GW(12)
+        LW(14)
+        GW(13)
+        LW(15)
+        MM(5)
+        GT(5)
+        QW(12)
+        QW(13)
+        QC(2)
+        PM(2)
+        EV(2, 0)
+        EV(2, 1)
+        EV(2, 2)
+        GW(14)
+        GW(15)
+        MM(6)
+        GT(6)
+        QW(14)
+        QW(15)
+        QC(3)
+        PM(3)
+        EV(3, 0)
+        EV(3, 1)
+        EV(3, 2)
+        MM(7)
+        GT(7)
+        QC(4)
+        PM(4)
+        EV(4, 0)
+        EV(4, 1)
+        EV(4, 2)
+        SC(1, 0)
+        SC(1, 1)
+        SC(1, 2)
+        SC(2, 0)
+        SC(2, 1)
+        SC(2, 2)
+        SC(3, 0)
+        SC(3, 1)
+        SC(3, 2)
+        SC(4, 0)
+        SC(4, 1)
+        SC(4, 2)
+        ST(0)
+        ST(1)
+        ST(2)

from contextlib import ExitStack

import concourse.mybir as mybir

K, T, E, C, N, M = 1024, 1280, 8, 128, 512, 384
SLOTS = E * C
FLOPS = 2 * SLOTS * K * N + 2 * T * N * M
BYTES = 4 * (K * T + E * K * N + N * M + SLOTS + M * T) + 2 * SLOTS

F32 = mybir.dt.float32
BF16 = mybir.dt.bfloat16
U32 = mybir.dt.uint32
U16 = mybir.dt.uint16
U8 = mybir.dt.uint8
FP8X4 = mybir.dt.float8_e4m3fn_x4
ADD = mybir.AluOpType.add
MULT = mybir.AluOpType.mult
COPY = mybir.ActivationFunctionType.Copy

P = 128
PACK = 4
KP = P * PACK
PASSES = K // KP
GATHER = 512
XRAW, XBF, WRAW, WBF, WQ = 4, 3, 5, 4, 4
X_CHUNKS = ((0, 0, 256), (0, 256, 768), (0, 768, 1280), (1, 0, 512), (1, 512, 1024), (1, 1024, 1280))
X_ENGINE = 'vvsvsv'
W_ENGINE = 'ssssssssssssssss'
WP_ENGINE = 's'
LAST_ENGINE = 'sssssssssssssss'
GROUPS = ((0, 2), (2, 2), (4, 2), (6, 1), (7, 1))
CUTS = ((0, 256), (256, 512), (512, 704), (704, 864), (864, 1024))
TURN_ENGINE = 'ssssssss'
SPLIT = {"p": 192, "q": 128, "r": 256}
GROUP_OF = {0: (0, 0, 2), 1: (0, 0, 2), 2: (1, 2, 2), 3: (1, 2, 2), 4: (2, 4, 2), 5: (2, 4, 2), 6: (3, 6, 1), 7: (4, 7, 1)}


def tile_moe_nxt_lin_none_kernel(tc, xT, w, wp, gate, offs, out):
    nc = tc.nc
    with ExitStack() as ctx:
        keep = ctx.enter_context(tc.tile_pool(name="keep", bufs=1))
        xraw = ctx.enter_context(tc.tile_pool(name="xraw", bufs=XRAW))
        xbf = ctx.enter_context(tc.tile_pool(name="xbf", bufs=XBF))
        wraw = ctx.enter_context(tc.tile_pool(name="wraw", bufs=WRAW))
        wbf = ctx.enter_context(tc.tile_pool(name="wbf", bufs=WBF))
        wq = ctx.enter_context(tc.tile_pool(name="wq", bufs=WQ))
        cpool = ctx.enter_context(tc.tile_pool(name="c", bufs=2))
        ypsum = ctx.enter_context(tc.psum_pool(name="ypsum", bufs=3))
        opsum = ctx.enter_context(tc.psum_pool(name="opsum", bufs=2))

        offsets = keep.tile([P, SLOTS // 16], U16, name="offsets")
        nc.sync.dma_start(offsets[:], offs)

        xcodes = [keep.tile([P, T], U32, align_bytes=64, name="xcodes%d" % a) for a in range(PASSES)]
        xscales = keep.tile([P, T], U8, align_bytes=64, name="xscales")
        gcodes = [keep.tile([P, SLOTS], U32, align_bytes=64, name="gcodes%d" % a) for a in range(PASSES)]
        gscales = keep.tile([P, SLOTS], U8, align_bytes=64, name="gscales")
        gates = keep.tile([P, SLOTS], F32, name="gates")
        wpraw = keep.tile([P, PACK, M], F32, name="wpraw")
        wpbf = keep.tile([P, M, PACK], BF16, align_bytes=64, name="wpbf")
        wpcodes = keep.tile([P, M], U32, align_bytes=64, name="wpcodes")
        wpscales = keep.tile([P, M], U8, align_bytes=64, name="wpscales")
        oslots = [keep.tile([P, SLOTS], F32, name="oslots%d" % f) for f in range(M // P)]
        windows = [keep.tile([P, T], F32, name="window%d" % f) for f in range(M // P)]

        nc.gpsimd.memset(xscales[:], 0)
        for f in range(M // P):
            nc.gpsimd.memset(windows[f][:], 0.0)

        x_tiles = {}
        x_parts = {}
        raw_tiles = {}
        grouped_tiles = {}
        quantized = {}
        products = {}
        gated = {}
        ccodes_of = {}
        projected = {}

        def copy(engine, dst, src):
            if engine == "v":
                nc.vector.tensor_copy(out=dst, in_=src)
            elif engine == "g":
                nc.gpsimd.tensor_scalar(out=dst, in0=src, scalar1=1.0, scalar2=0.0, op0=MULT, op1=ADD)
            else:
                nc.scalar.activation(out=dst, in_=src, func=COPY)

        def LX(i):
            a, t0, t1 = X_CHUNKS[i]
            xr = xraw.tile([P, PACK, t1 - t0], F32, name="xr")
            nc.sync.dma_start(xr[:], xT[a * KP:(a + 1) * KP, t0:t1].rearrange("(p j) t -> p j t", j=PACK))
            x_parts[i] = xr

        def GX(i):
            a, t0, t1 = X_CHUNKS[i]
            xb = xbf.tile([P, (t1 - t0) * PACK], BF16, align_bytes=64, name="xb")
            copy(
                X_ENGINE[i],
                xb[:].rearrange("p (c i j) -> p c j i", i=4, j=PACK),
                x_parts.pop(i)[:].rearrange("p j (c i) -> p c j i", i=4),
            )
            x_tiles[i] = xb

        def QX(i):
            a, t0, t1 = X_CHUNKS[i]
            nc.vector.quantize_mx(
                out=xcodes[a][:, t0:t1].bitcast(FP8X4), scales=xscales[PACK * a:P, t0:t1], in_=x_tiles.pop(i)[:]
            )

        def GA(a, g):
            nc.vector.tensor_copy(
                out=gcodes[a][:, g * GATHER:(g + 1) * GATHER],
                in_=xcodes[a][:].indirect(offsets[:, g * GATHER // 16:(g + 1) * GATHER // 16]),
            )

        def GS(g):
            nc.vector.tensor_copy(
                out=gscales[:, g * GATHER:(g + 1) * GATHER],
                in_=xscales[:].indirect(offsets[:, g * GATHER // 16:(g + 1) * GATHER // 16]),
            )

        def LG():
            nc.sync.dma_start(gates[:], gate[0:P, :])

        def LP():
            nc.sync.dma_start(wpraw[:], wp.rearrange("(q r) f -> q r f", r=PACK))

        def GP():
            copy(
                WP_ENGINE,
                wpbf[:].rearrange("q (c i) r -> q c r i", i=4),
                wpraw[:].rearrange("q r (c i) -> q c r i", i=4),
            )

        def QP(i):
            f0, f1 = ((0, 256), (256, 384))[i]
            nc.vector.quantize_mx(
                out=wpcodes[:, f0:f1].bitcast(FP8X4),
                scales=wpscales[:, f0:f1],
                in_=wpbf[:, f0:f1, :].rearrange("p f r -> p (f r)"),
            )

        def LW(k):
            e, a = divmod(k, PASSES)
            raw = wraw.tile([P, PACK, N], F32, name="raw")
            nc.sync.dma_start(raw[:], w[e, a * KP:(a + 1) * KP, :].rearrange("(p j) n -> p j n", j=PACK))
            raw_tiles[k] = raw

        def GW(k):
            grouped = wbf.tile([P, N * PACK], BF16, align_bytes=64, name="grouped")
            dst = grouped[:].rearrange("p (t m j) -> p m j t", t=PACK, j=PACK)
            src = raw_tiles.pop(k)[:].rearrange("p j (m t) -> p m j t", t=PACK)
            copy(W_ENGINE[k], dst, src)
            grouped_tiles[k] = grouped

        def QW(k):
            codes = wq.tile([P, N], U32, align_bytes=64, name="codes")
            scales = wq.tile([P, N], U8, align_bytes=64, name="scales")
            nc.vector.quantize_mx(out=codes[:].bitcast(FP8X4), scales=scales[:], in_=grouped_tiles.pop(k)[:])
            quantized[k] = codes, scales

        def MM(e):
            y = ypsum.tile([P, PACK, C], F32, name="y")
            for t in range(PACK):
                for a in range(PASSES):
                    codes, scales = quantized[e * PASSES + a]
                    nc.tensor.matmul_mx(
                        out=y[:, t, :],
                        lhsT=codes[:, t * P:(t + 1) * P].bitcast(FP8X4),
                        lhsT_scale=scales[:, t * P:(t + 1) * P],
                        rhs=gcodes[a][:, e * C:(e + 1) * C].bitcast(FP8X4),
                        rhs_scale=gscales[PACK * a:P, e * C:(e + 1) * C],
                        start=(a == 0),
                        stop=(a == PASSES - 1),
                    )
            products[e] = y

        def GT(e):
            gi, first, size = GROUP_OF[e]
            if gi not in gated:
                cb = cpool.tile([P, size * C, PACK], BF16, align_bytes=64, name="cb")
                gated[gi] = cb
            i = e - first
            nc.vector.tensor_tensor(
                out=gated[gi][:, i * C:(i + 1) * C, :],
                in0=products.pop(e)[:].rearrange("p t s -> p s t"),
                in1=gates[:, e * C:(e + 1) * C].unsqueeze(2).to_broadcast([P, C, PACK]),
                op=MULT,
            )

        def QC(gi):
            width = GROUPS[gi][1] * C
            ccodes = cpool.tile([P, width], U32, align_bytes=64, name="ccodes")
            cscales = cpool.tile([P, width], U8, align_bytes=64, name="cscales")
            nc.vector.quantize_mx(
                out=ccodes[:].bitcast(FP8X4), scales=cscales[:], in_=gated[gi][:].rearrange("p s r -> p (s r)")
            )
            ccodes_of[gi] = ccodes, cscales

        def PM(gi):
            width = GROUPS[gi][1] * C
            ccodes, cscales = ccodes_of.pop(gi)
            o = opsum.tile([P, 4, 2 * C], F32, name="o")
            for f in range(M // P):
                nc.tensor.matmul_mx(
                    out=o[:, f, 0:width],
                    lhsT=wpcodes[:, f * P:(f + 1) * P].bitcast(FP8X4),
                    lhsT_scale=wpscales[:, f * P:(f + 1) * P],
                    rhs=ccodes[:].bitcast(FP8X4),
                    rhs_scale=cscales[:],
                    start=True,
                    stop=True,
                )
            projected[gi] = o

        def EV(gi, f):
            first, size = GROUPS[gi]
            s0, s1 = first * C, (first + size) * C
            copy(LAST_ENGINE[gi * 3 + f], oslots[f][:, s0:s1], projected[gi][:, f, 0:s1 - s0])

        def SC(i, f):
            a0, a1 = CUTS[i]
            nc.vector.tensor_copy(
                out=windows[f][:].indirect(offsets[:, a0 // 16:a1 // 16]), in_=oslots[f][:, a0:a1]
            )

        def ST(f):
            nc.sync.dma_start(out[f * P:(f + 1) * P, :], windows[f][:])

        LX(0)
        GX(0)
        QX(0)
        LX(2)
        GX(2)
        QX(2)
        LX(1)
        GX(1)
        QX(1)
        GA(0, 0)
        GA(0, 1)
        LX(4)
        GX(4)
        QX(4)
        LX(3)
        GX(3)
        QX(3)
        LW(0)
        GW(0)
        LX(5)
        GX(5)
        QX(5)
        GA(1, 0)
        GA(1, 1)
        LW(1)
        LG()
        LP()
        LW(2)
        LW(3)
        LW(4)
        GS(0)
        GS(1)
        GW(1)
        QW(0)
        QW(1)
        GW(2)
        GW(3)
        LW(5)
        GP()
        QP(0)
        QP(1)
        MM(0)
        GT(0)
        QW(2)
        QW(3)
        GW(4)
        LW(6)
        GW(5)
        LW(7)
        MM(1)
        GT(1)
        QW(4)
        QW(5)
        QC(0)
        PM(0)
        EV(0, 0)
        EV(0, 1)
        EV(0, 2)
        GW(6)
        LW(8)
        GW(7)
        LW(9)
        MM(2)
        GT(2)
        QW(6)
        QW(7)
        GW(8)
        LW(10)
        GW(9)
        LW(11)
        MM(3)
        GT(3)
        QW(8)
        QW(9)
        QC(1)
        PM(1)
        EV(1, 0)
        EV(1, 1)
        EV(1, 2)
        GW(10)
        LW(12)
        GW(11)
        LW(13)
        MM(4)
        GT(4)
        QW(10)
        QW(11)
        SC(0, 0)
        SC(0, 1)
        SC(0, 2)
        GW(12)
        LW(14)
        GW(13)
        LW(15)
        MM(5)
        GT(5)
        QW(12)
        QW(13)
        QC(2)
        PM(2)
        EV(2, 0)
        EV(2, 1)
        EV(2, 2)
        GW(14)
        GW(15)
        MM(6)
        GT(6)
        QW(14)
        QW(15)
        QC(3)
        PM(3)
        EV(3, 0)
        EV(3, 1)
        EV(3, 2)
        MM(7)
        GT(7)
        QC(4)
        PM(4)
        EV(4, 0)
        EV(4, 1)
        EV(4, 2)
        SC(1, 0)
        SC(1, 1)
        SC(1, 2)
        SC(2, 0)
        SC(2, 1)
        SC(2, 2)
        SC(3, 0)
        SC(3, 1)
        SC(3, 2)
        SC(4, 0)
        SC(4, 1)
        SC(4, 2)
        ST(0)
        ST(1)
        ST(2)
